import numpy as np
import ml_dtypes


def mxq(x, axis, fmt="e4m3"):
    dtype, down = {"e4m3": (ml_dtypes.float8_e4m3fn, 7), "e5m2": (ml_dtypes.float8_e5m2, 14)}[fmt]
    v = np.moveaxis(np.asarray(x, np.float32).astype(ml_dtypes.bfloat16).astype(np.float64), axis, -1)
    blocks = v.reshape(v.shape[:-1] + (-1, 32))
    amax = np.abs(blocks).max(-1, keepdims=True)
    byte = np.maximum(np.where(amax > 0, np.frexp(amax)[1] - 1 + 127, 0) - down, 1)
    scale = np.exp2(byte - 127.0)
    codes = (blocks / scale).astype(np.float32).astype(dtype).astype(np.float64)
    return np.moveaxis((codes * scale).reshape(v.shape), -1, axis)


WIDE = False


def mx_kscale(k):
    if not WIDE:
        return np.ones(k)
    levels = np.array([10, -10, 5, -5, 0])
    if k % 512:
        return np.exp2(np.random.permutation(np.resize(levels, k // 32))).repeat(32)
    a = np.empty((k // 512, 16))
    for p in range(k // 512):
        a[p, :8] = np.random.permutation(np.resize(levels, 8))
        for g in range(8):
            far = levels[np.abs(levels - a[p, g]) >= 10]
            a[p, g + 8] = far[np.random.randint(len(far))]
    return np.exp2(a.ravel()).repeat(32)


def f64(x):
    return np.asarray(x).astype(np.float64)


def striped(idx):
    return np.tile(idx.reshape(-1, 16).T, (8, 1)).astype(np.uint16)


def unstriped(offs):
    return offs[:16].T.reshape(-1).astype(np.int64)


def striped8(idx):
    return np.concatenate([x.reshape(-1, 16).T for x in idx]).astype(np.uint16)


def runs(offs, k):
    lists = np.stack([offs[16 * r : 16 * r + 16].T.reshape(-1) for r in range(8)]).astype(np.int64)
    return lists[np.arange(k) % 512 // 64]


def pack_weight(w):
    k, n = w.shape
    w = f64(np.asarray(w, np.float32).astype(ml_dtypes.bfloat16)).reshape(k // 32, 32, n)
    amax = np.abs(w).max(1)
    byte = np.clip(np.where(amax > 0, np.frexp(amax)[1] - 1 + 127 - 7, 1), 1, 254)
    scaled = (w * np.exp2(127.0 - byte)[:, None, :]).reshape(k, n).astype(np.float32)
    words = np.ascontiguousarray(scaled.reshape(k // 512, 128, 4, n).transpose(0, 1, 3, 2)).astype(ml_dtypes.float8_e4m3fn).view(np.uint8)
    return words, np.ascontiguousarray(byte.astype(np.uint8).reshape(k // 512, 16, n))


def unpack_weight(words, scales):
    g, p, n, _ = words.shape
    vals = np.ascontiguousarray(words).view(ml_dtypes.float8_e4m3fn).astype(np.float64) * np.repeat(np.exp2(scales.astype(np.float64) - 127.0), 8, axis=1)[..., None]
    return vals.transpose(0, 1, 3, 2).reshape(g * 512, n)

def planes(y):
    n, m = y.shape
    v = y.astype(np.float32).astype(ml_dtypes.bfloat16).astype(np.float64).reshape(n // 32, 32, m)
    top = np.abs(v).max(1)
    byte = np.clip(np.where(top > 0, np.frexp(top)[1] - 1 + 127 - 7, 1), 1, 254)
    codes = (v * np.exp2(127.0 - byte)[:, None, :]).reshape(n, m).astype(np.float32).astype(ml_dtypes.float8_e4m3fn).view(np.uint8)
    words = codes.reshape(n // 512, 128, 4, m).transpose(0, 1, 3, 2)
    return np.ascontiguousarray(words), np.ascontiguousarray(byte.astype(np.uint8).reshape(n // 512, 16, m))


K, T, S, N, G, H = 512, 2048, 512, 512, 2048, 512


def setup_inputs():
    n = np.random.standard_normal
    s = mx_kscale(K)[:, None]
    u = mx_kscale(S)
    packed_xT = pack_weight(n((K, T)) * s)
    packed_dT = pack_weight(n((K, G)) / s)
    packed_w1 = pack_weight(n((H, N)) / np.sqrt(2 * H) / u[:, None])
    packed_w2 = pack_weight(n((K, N)) / np.sqrt(2 * K) / s)
    return {
        "x_words": packed_xT[0],
        "x_scales": packed_xT[1],
        "d_words": packed_dT[0],
        "d_scales": packed_dT[1],
        "gn": (np.random.uniform(0.5, 1.5, (H, 1)) * u[:, None]).astype(np.float32),
        "w1_words": packed_w1[0],
        "w1_scales": packed_w1[1],
        "w2_words": packed_w2[0],
        "w2_scales": packed_w2[1],
        "offs": striped(np.random.permutation(T)[:S]),
        "k1": striped8(np.random.randint(0, G, (8, H))),
        "n1": striped8(np.stack([np.random.permutation(S) for _ in range(8)])),
        "n2": striped8(np.stack([np.random.permutation(S) for _ in range(8)])),
        "two": striped(np.random.permutation(T)[:S]),
        "n3": striped(np.random.randint(0, S, G)),
    }


def reference(x_words, x_scales, d_words, d_scales, gn, w1_words, w1_scales, w2_words, w2_scales, offs, k1, n1, n2, two, n3):
    d_k1 = unpack_weight(d_words, d_scales)[np.arange(K)[:, None], runs(k1, K)]
    xq = unpack_weight(x_words, x_scales)[:, unstriped(offs)]
    s = 0.0625 * (d_k1.T @ xq)
    z = f64(gn) * ((s * (s[np.arange(H)[:, None], runs(n1, H)])) * (np.tanh(s[np.arange(H)[:, None], runs(n2, H)])))
    x_two = unpack_weight(x_words, x_scales)[:, unstriped(two)]
    h = unpack_weight(w1_words, w1_scales).T @ mxq(z, 0, "e4m3") + unpack_weight(w2_words, w2_scales).T @ x_two
    mb = h[:, unstriped(n3)]
    mx = mb.reshape(N, S, 4).max(axis=2)
    out_0 = h - mx
    return (out_0,) + planes(out_0)

@@ -1,0 +1,224 @@
+from contextlib import ExitStack
+
+import concourse.mybir as mybir
+
+F32 = mybir.dt.float32
+BF16 = mybir.dt.bfloat16
+U32 = mybir.dt.uint32
+I32 = mybir.dt.int32
+U16 = mybir.dt.uint16
+U8 = mybir.dt.uint8
+FP8X4 = mybir.dt.float8_e4m3fn_x4
+ALU = mybir.AluOpType
+ACT = mybir.ActivationFunctionType
+
+P = 128
+PACK = 4
+S = 512
+TABLE = 2048
+SCORE_SCALE = 0.0625
+BANK_COLS = 128
+Z_CHUNKS = ((0, 256), (256, 128), (384, 128))
+H_WINDOW = S + 16
+OUT_CHUNKS = ((0, 128), (128, 128), (256, 128), (384, 64), (448, 64))
+FLOPS = 3 * 2 * 512 * 512 * 512
+
+
+def tile_picked_kmixcubegmaxd_none_po_kernel(
+    tc, x_words, x_scales, d_words, d_scales, gn, w1_words, w1_scales, w2_words, w2_scales,
+    offs, k1, n1, n2, two, n3, out_0, out_1, out_2,
+):
+    nc = tc.nc
+
+    def words_in_hbm(words):
+        return words[0].rearrange("p c r -> p (c r)").bitcast(I32)
+
+    with ExitStack() as ctx:
+        held = ctx.enter_context(tc.tile_pool(name="held", bufs=1))
+        psum = ctx.enter_context(tc.psum_pool(name="psum", bufs=1))
+
+        def load_list(src, name):
+            tile = held.tile(list(src.shape), U16, name=name)
+            nc.sync.dma_start(tile[:], src)
+            return tile
+
+        d_scale_table = held.tile([P, TABLE], U8, name="d_scale_table", tag="d_scales_then_w2_words", align_bytes=64)
+        x_scale_table = held.tile([P, TABLE], U8, name="x_scale_table", align_bytes=64)
+        nc.gpsimd.memset(x_scale_table[:].bitcast(I32), 0)
+
+        k1_list = load_list(k1, "k1_list")
+        d_scale_rows = d_scales[0].bitcast(I32)
+        nc.sync.dma_start(
+            d_scale_table[:].bitcast(I32), d_scale_rows.unsqueeze(1).to_broadcast([16, 8, TABLE // 4])
+        )
+        offs_list = load_list(offs, "offs_list")
+        d_word_table = held.tile([P, TABLE], U32, name="d_word_table", tag="d_then_w_words", align_bytes=64)
+        x_word_table = held.tile([P, TABLE], U32, name="x_word_table", align_bytes=64)
+        nc.sync.dma_start(d_word_table[:].bitcast(I32), words_in_hbm(d_words))
+        x_scale_rows = x_scales[0].bitcast(I32)
+        for q in range(4):
+            nc.sync.dma_start(x_scale_table[32 * q : 32 * q + 4, :].bitcast(I32), x_scale_rows[4 * q : 4 * q + 4, :])
+        nc.sync.dma_start(x_word_table[:].bitcast(I32), words_in_hbm(x_words))
+        two_list = load_list(two, "two_list")
+        n1_list = load_list(n1, "n1_list")
+        n2_list = load_list(n2, "n2_list")
+        n3_list = load_list(n3, "n3_list")
+        gain = held.tile([P, PACK], F32, name="gain")
+        nc.gpsimd.dma_start(gain[:], gn.rearrange("(p t) o -> p (t o)", t=PACK))
+
+        def gather_packed(table, offsets, dtype, name, tag=None):
+            picked = held.tile([P, S], dtype, name=name, tag=tag or name, align_bytes=64)
+            nc.vector.tensor_copy(picked[:], table[:].indirect(offsets[:]))
+            return picked
+
+        def dealt(tile):
+            return tile.rearrange("p (m t) -> p t m", t=PACK)
+
+        def by_tile(tile):
+            return tile.rearrange("p (t m) -> p t m", t=PACK)
+
+        key_scales_picked = gather_packed(d_scale_table, k1_list, U8, "key_scales_picked")
+        key_scales_dealt = held.tile([P, S], U8, name="key_scales_dealt", align_bytes=64)
+        nc.vector.tensor_copy(by_tile(key_scales_dealt[:]), dealt(key_scales_picked[:]))
+        key_scales = held.tile([P, S], U8, name="key_scales", align_bytes=64)
+        nc.vector.tensor_copy(key_scales[:].bitcast(I32), key_scales_dealt[:].bitcast(I32))
+        for r in range(1, 4):
+            nc.scalar.dma_start(key_scales[r:P:32, :].bitcast(I32), key_scales_dealt[8 * r : P : 32, :].bitcast(I32))
+        key_words_picked = gather_packed(d_word_table, k1_list, U32, "key_words_picked", tag="key_words_then_w_scales")
+        key_words = held.tile([P, S], U32, name="key_words", align_bytes=64)
+        nc.vector.tensor_copy(by_tile(key_words[:]), dealt(key_words_picked[:]))
+        xq_scales = gather_packed(x_scale_table, offs_list, U8, "xq_scales")
+        xq_words = gather_packed(x_word_table, offs_list, U32, "xq_words")
+
+        score_banks = [psum.tile([P, S], F32, name=f"score_bank{t}") for t in range(PACK)]
+        for t in range(PACK):
+            cols = slice(P * t, P * (t + 1))
+            nc.tensor.matmul_mx(
+                out=score_banks[t][:], lhsT=key_words[:, cols].bitcast(FP8X4), lhsT_scale=key_scales[:, cols],
+                rhs=xq_words[:].bitcast(FP8X4), rhs_scale=xq_scales[:], start=True, stop=True,
+            )
+
+        x2_scales = gather_packed(x_scale_table, two_list, U8, "x2_scales")
+        x2_words = gather_packed(x_word_table, two_list, U32, "x2_words")
+
+        w2_raw = held.tile([P, S], U32, name="w2_raw", tag="d_scales_then_w2_words", align_bytes=64)
+        w1_raw = held.tile([P, S], U32, name="w1_raw", tag="d_then_w_words", align_bytes=64)
+        nc.gpsimd.dma_start(w2_raw[:].bitcast(I32), words_in_hbm(w2_words))
+        nc.gpsimd.dma_start(w1_raw[:].bitcast(I32), words_in_hbm(w1_words))
+        w1_dealt = held.tile([P, S], U32, name="w1_dealt", align_bytes=64)
+        w2_dealt = held.tile([P, S], U32, name="w2_dealt", align_bytes=64)
+        nc.scalar.copy(by_tile(w2_dealt[:]), dealt(w2_raw[:]))
+        nc.scalar.copy(by_tile(w1_dealt[:]), dealt(w1_raw[:]))
+        w_scales_raw = held.tile([P, S], U8, name="w_scales_raw", tag="key_words_then_w_scales", align_bytes=64)
+        nc.gpsimd.memset(w_scales_raw[:], 0)
+        for first, scales in ((0, w1_scales), (4, w2_scales)):
+            rows = scales[0].bitcast(I32)
+            for q in range(4):
+                nc.sync.dma_start(
+                    w_scales_raw[32 * q + first : 32 * q + first + 4, :].bitcast(I32), rows[4 * q : 4 * q + 4, :]
+                )
+        w_scales = held.tile([P, S], U8, name="w_scales", align_bytes=64)
+        nc.gpsimd.tensor_copy(by_tile(w_scales[:]), dealt(w_scales_raw[:]))
+
+        n_banks = S // BANK_COLS
+        h_banks = [psum.tile([P, PACK, BANK_COLS], F32, name=f"h_bank{b}") for b in range(n_banks)]
+        for b in range(n_banks):
+            cols = slice(BANK_COLS * b, BANK_COLS * (b + 1))
+            for t in range(PACK):
+                rows = slice(P * t, P * (t + 1))
+                nc.tensor.matmul_mx(
+                    out=h_banks[b][:, t, :], lhsT=w2_dealt[:, rows].bitcast(FP8X4), lhsT_scale=w_scales[4:P, rows],
+                    rhs=x2_words[:, cols].bitcast(FP8X4), rhs_scale=x2_scales[:, cols], start=(t == 0), stop=False,
+                )
+
+        scaled_gain = held.tile([P, PACK], F32, name="scaled_gain")
+        nc.gpsimd.tensor_scalar(scaled_gain[:], gain[:], SCORE_SCALE, 0.0, ALU.mult, ALU.add)
+        s_rows = [held.tile([P, S], F32, name=f"s_rows{t}") for t in range(PACK)]
+        tanh_rows = [held.tile([P, S], F32, name=f"tanh_rows{t}") for t in range(PACK)]
+        h_rows = [held.tile([P, H_WINDOW], F32, name=f"h_rows{t}") for t in range(PACK)]
+        for t in range(PACK):
+            nc.gpsimd.memset(h_rows[t][:, S:], 0.0)
+
+        def round_interleaved(engine_copy, values, width, name):
+            rounded = held.tile([P, width * PACK], BF16, name=name, align_bytes=64)
+            engine_copy(
+                rounded[:].rearrange("p (c i t) -> p c t i", i=4, t=PACK),
+                values[:].rearrange("p t (c i) -> p c t i", i=4),
+            )
+            return rounded
+
+        for n, (start, width) in enumerate(Z_CHUNKS):
+            cols = slice(start, start + width)
+            entries = slice(start // 16, (start + width) // 16)
+            z_values = held.tile([P, PACK, width], F32, name=f"z_values{n}")
+            for t in range(PACK):
+                if n == 0:
+                    if t < 2:
+                        nc.scalar.activation(s_rows[t][:], score_banks[t][:], ACT.Copy, scale=SCORE_SCALE)
+                    else:
+                        nc.vector.tensor_scalar(s_rows[t][:], score_banks[t][:], SCORE_SCALE, None, ALU.mult)
+                    nc.scalar.activation(tanh_rows[t][:], score_banks[t][:], ACT.Tanh, scale=SCORE_SCALE)
+                s_at_n1 = held.tile([P, width], F32, name=f"s_at_n1_{n}_{t}")
+                if (n, t) == (1, 0):
+                    nc.vector.tensor_copy(s_at_n1[:], s_rows[t][:].indirect(n1_list[:, entries]))
+                else:
+                    nc.scalar.activation(s_at_n1[:], s_rows[t][:].indirect(n1_list[:, entries]), ACT.Copy)
+                pair = held.tile([P, width], F32, name=f"pair_{n}_{t}")
+                nc.vector.tensor_tensor(pair[:], tanh_rows[t][:].indirect(n2_list[:, entries]), s_at_n1[:], ALU.mult)
+                nc.vector.scalar_tensor_tensor(
+                    z_values[:, t, :], score_banks[t][:, cols], scaled_gain[:, t : t + 1], pair[:], ALU.mult, ALU.mult
+                )
+            z_rounded = round_interleaved(
+                nc.vector.tensor_copy if n == len(Z_CHUNKS) - 1 else nc.scalar.copy, z_values, width, f"z_rounded{n}")
+            z_words = held.tile([P, width], U32, name=f"z_words{n}", align_bytes=64)
+            z_scales = held.tile([P, width], U8, name=f"z_scales{n}", align_bytes=64)
+            nc.vector.quantize_mx(out=z_words[:].bitcast(FP8X4), scales=z_scales[:], in_=z_rounded[:])
+            for b in range(start // BANK_COLS, (start + width) // BANK_COLS):
+                part = slice(BANK_COLS * b - start, BANK_COLS * (b + 1) - start)
+                for t in range(PACK):
+                    rows = slice(P * t, P * (t + 1))
+                    nc.tensor.matmul_mx(
+                        out=h_banks[b][:, t, :], lhsT=w1_dealt[:, rows].bitcast(FP8X4), lhsT_scale=w_scales[:, rows],
+                        rhs=z_words[:, part].bitcast(FP8X4), rhs_scale=z_scales[:, part],
+                        start=False, stop=(t == PACK - 1),
+                    )
+        for b in range(n_banks):
+            for t in range(PACK):
+                copy_out = nc.vector.tensor_copy if (b == n_banks - 1 and t > 0) else nc.scalar.copy
+                copy_out(h_rows[t][:, BANK_COLS * b : BANK_COLS * (b + 1)], h_banks[b][:, t, :])
+
+        out_rows = out_0.rearrange("(p t) j -> p t j", t=PACK)
+        out_words_hbm = words_in_hbm(out_1)
+        out_scales = held.tile([P, S], U8, name="out_scales", align_bytes=64)
+        for n, (start, width) in enumerate(OUT_CHUNKS):
+            cols = slice(start, start + width)
+            entries = slice(start // 4, (start + width) // 4)
+            members = held.tile([P, PACK, 4 * width], F32, name=f"members{n}")
+            for t in range(PACK):
+                looked_up = h_rows[t][:].indirect(n3_list[:, entries])
+                if t == PACK - 1:
+                    nc.vector.tensor_copy(members[:, t, :], looked_up)
+                else:
+                    nc.scalar.activation(members[:, t, :], looked_up, ACT.Copy)
+            quads = members[:].rearrange("p t (j m) -> p (t j) m", m=4)
+            pair_max = held.tile([P, PACK * width, 2], F32, name=f"pair_max{n}")
+            nc.vector.tensor_tensor(pair_max[:], quads[:, :, 0:2], quads[:, :, 2:4], ALU.max)
+            largest = held.tile([P, PACK * width], F32, name=f"largest{n}")
+            nc.vector.tensor_tensor(largest[:], pair_max[:, :, 0], pair_max[:, :, 1], ALU.max)
+            result = held.tile([P, PACK, width], F32, name=f"result{n}")
+            in_bank = slice(start % BANK_COLS, start % BANK_COLS + width)
+            nc.vector.tensor_tensor(
+                result[:], h_banks[start // BANK_COLS][:, :, in_bank],
+                largest[:].rearrange("p (t j) -> p t j", t=PACK), ALU.subtract,
+            )
+            nc.sync.dma_start(out_rows[:, :, cols], result[:])
+            rounded = round_interleaved(
+                nc.vector.tensor_copy if n < 2 else nc.scalar.copy, result, width, f"out_rounded{n}"
+            )
+            out_words = held.tile([P, width], U32, name=f"out_words{n}", align_bytes=64)
+            nc.vector.quantize_mx(out=out_words[:].bitcast(FP8X4), scales=out_scales[:, cols], in_=rounded[:])
+            nc.sync.dma_start(out_words_hbm[:, cols], out_words[:].bitcast(I32))
+        out_scale_rows = out_2[0].bitcast(I32)
+        for q in range(4):
+            queue = nc.scalar if q % 2 else nc.sync
+            queue.dma_start(out_scale_rows[4 * q : 4 * q + 4, :], out_scales[32 * q : 32 * q + 4, :].bitcast(I32))

@@ -52,7 +52,7 @@ def tile_picked_kmixcubegmaxd_none_po_kernel(
             d_scale_table[:].bitcast(I32), d_scale_rows.unsqueeze(1).to_broadcast([16, 8, TABLE // 4])
         )
         offs_list = load_list(offs, "offs_list")
-        d_word_table = held.tile([P, TABLE], U32, name="d_word_table", tag="d_then_w_words", align_bytes=64)
+        d_word_table = held.tile([P, TABLE], U32, name="d_word_table", align_bytes=64)
         x_word_table = held.tile([P, TABLE], U32, name="x_word_table", align_bytes=64)
         nc.sync.dma_start(d_word_table[:].bitcast(I32), words_in_hbm(d_words))
         x_scale_rows = x_scales[0].bitcast(I32)
@@ -64,7 +64,7 @@ def tile_picked_kmixcubegmaxd_none_po_kernel(
         n2_list = load_list(n2, "n2_list")
         n3_list = load_list(n3, "n3_list")
         gain = held.tile([P, PACK], F32, name="gain")
-        nc.gpsimd.dma_start(gain[:], gn.rearrange("(p t) o -> p (t o)", t=PACK))
+        nc.sync.dma_start(gain[:], gn.rearrange("(p t) o -> p (t o)", t=PACK))
 
         def gather_packed(table, offsets, dtype, name, tag=None):
             picked = held.tile([P, S], dtype, name=name, tag=tag or name, align_bytes=64)
@@ -77,8 +77,13 @@ def tile_picked_kmixcubegmaxd_none_po_kernel(
         def by_tile(tile):
             return tile.rearrange("p (t m) -> p t m", t=PACK)
 
-        key_scales_picked = gather_packed(d_scale_table, k1_list, U8, "key_scales_picked")
-        key_scales_dealt = held.tile([P, S], U8, name="key_scales_dealt", align_bytes=64)
+        def deal_words(engine_copy, dst, src):
+            engine_copy(
+                dst[:].rearrange("p (t c i) -> p c t i", t=PACK, i=4), src[:].rearrange("p (c i t) -> p c t i", t=PACK, i=4)
+            )
+
+        key_scales_picked = gather_packed(d_scale_table, k1_list, U8, "key_scales_picked", tag="key_scales_then_w1_words")
+        key_scales_dealt = held.tile([P, S], U8, name="key_scales_dealt", tag="key_then_x2_scales", align_bytes=64)
         nc.vector.tensor_copy(by_tile(key_scales_dealt[:]), dealt(key_scales_picked[:]))
         key_scales = held.tile([P, S], U8, name="key_scales", align_bytes=64)
         nc.vector.tensor_copy(key_scales[:].bitcast(I32), key_scales_dealt[:].bitcast(I32))
@@ -86,7 +91,7 @@ def tile_picked_kmixcubegmaxd_none_po_kernel(
             nc.scalar.dma_start(key_scales[r:P:32, :].bitcast(I32), key_scales_dealt[8 * r : P : 32, :].bitcast(I32))
         key_words_picked = gather_packed(d_word_table, k1_list, U32, "key_words_picked", tag="key_words_then_w_scales")
         key_words = held.tile([P, S], U32, name="key_words", align_bytes=64)
-        nc.vector.tensor_copy(by_tile(key_words[:]), dealt(key_words_picked[:]))
+        deal_words(nc.vector.tensor_copy, key_words, key_words_picked)
         xq_scales = gather_packed(x_scale_table, offs_list, U8, "xq_scales")
         xq_words = gather_packed(x_word_table, offs_list, U32, "xq_words")
 
@@ -98,17 +103,17 @@ def tile_picked_kmixcubegmaxd_none_po_kernel(
                 rhs=xq_words[:].bitcast(FP8X4), rhs_scale=xq_scales[:], start=True, stop=True,
             )
 
-        x2_scales = gather_packed(x_scale_table, two_list, U8, "x2_scales")
+        x2_scales = gather_packed(x_scale_table, two_list, U8, "x2_scales", tag="key_then_x2_scales")
         x2_words = gather_packed(x_word_table, two_list, U32, "x2_words")
 
         w2_raw = held.tile([P, S], U32, name="w2_raw", tag="d_scales_then_w2_words", align_bytes=64)
-        w1_raw = held.tile([P, S], U32, name="w1_raw", tag="d_then_w_words", align_bytes=64)
+        w1_raw = held.tile([P, S], U32, name="w1_raw", tag="key_scales_then_w1_words", align_bytes=64)
         nc.gpsimd.dma_start(w2_raw[:].bitcast(I32), words_in_hbm(w2_words))
         nc.gpsimd.dma_start(w1_raw[:].bitcast(I32), words_in_hbm(w1_words))
         w1_dealt = held.tile([P, S], U32, name="w1_dealt", align_bytes=64)
         w2_dealt = held.tile([P, S], U32, name="w2_dealt", align_bytes=64)
-        nc.scalar.copy(by_tile(w2_dealt[:]), dealt(w2_raw[:]))
-        nc.scalar.copy(by_tile(w1_dealt[:]), dealt(w1_raw[:]))
+        deal_words(nc.scalar.copy, w2_dealt, w2_raw)
+        deal_words(nc.scalar.copy, w1_dealt, w1_raw)
         w_scales_raw = held.tile([P, S], U8, name="w_scales_raw", tag="key_words_then_w_scales", align_bytes=64)
         nc.gpsimd.memset(w_scales_raw[:], 0)
         for first, scales in ((0, w1_scales), (4, w2_scales)):
@@ -142,8 +147,8 @@ def tile_picked_kmixcubegmaxd_none_po_kernel(
         def round_interleaved(engine_copy, values, width, name):
             rounded = held.tile([P, width * PACK], BF16, name=name, align_bytes=64)
             engine_copy(
-                rounded[:].rearrange("p (c i t) -> p c t i", i=4, t=PACK),
-                values[:].rearrange("p t (c i) -> p c t i", i=4),
+                rounded[:].rearrange("p (j t) -> p j t", t=PACK),
+                values[:].rearrange("p t j -> p j t"),
             )
             return rounded
 
@@ -200,11 +205,15 @@ def tile_picked_kmixcubegmaxd_none_po_kernel(
                     nc.vector.tensor_copy(members[:, t, :], looked_up)
                 else:
                     nc.scalar.activation(members[:, t, :], looked_up, ACT.Copy)
-            quads = members[:].rearrange("p t (j m) -> p (t j) m", m=4)
-            pair_max = held.tile([P, PACK * width, 2], F32, name=f"pair_max{n}")
-            nc.vector.tensor_tensor(pair_max[:], quads[:, :, 0:2], quads[:, :, 2:4], ALU.max)
+            quads = members[:].rearrange("p t (u v m) -> p (t u) v m", v=2, m=4)
+            pair_max = held.tile([P, PACK * width // 2, 2, 2], F32, name=f"pair_max{n}")
+            nc.vector.tensor_tensor(
+                pair_max[:].rearrange("p u m v -> p u v m"), quads[:, :, :, 0:2], quads[:, :, :, 2:4], ALU.max
+            )
             largest = held.tile([P, PACK * width], F32, name=f"largest{n}")
-            nc.vector.tensor_tensor(largest[:], pair_max[:, :, 0], pair_max[:, :, 1], ALU.max)
+            nc.vector.tensor_tensor(
+                largest[:].rearrange("p (u v) -> p u v", v=2), pair_max[:, :, 0, :], pair_max[:, :, 1, :], ALU.max
+            )
             result = held.tile([P, PACK, width], F32, name=f"result{n}")
             in_bank = slice(start % BANK_COLS, start % BANK_COLS + width)
             nc.vector.tensor_tensor(

from contextlib import ExitStack

import concourse.mybir as mybir

F32 = mybir.dt.float32
BF16 = mybir.dt.bfloat16
U32 = mybir.dt.uint32
I32 = mybir.dt.int32
U16 = mybir.dt.uint16
U8 = mybir.dt.uint8
FP8X4 = mybir.dt.float8_e4m3fn_x4
ALU = mybir.AluOpType
ACT = mybir.ActivationFunctionType

P = 128
PACK = 4
S = 512
TABLE = 2048
SCORE_SCALE = 0.0625
BANK_COLS = 128
Z_CHUNKS = ((0, 256), (256, 128), (384, 128))
H_WINDOW = S + 16
OUT_CHUNKS = ((0, 128), (128, 128), (256, 128), (384, 64), (448, 64))
FLOPS = 3 * 2 * 512 * 512 * 512


def tile_picked_kmixcubegmaxd_none_po_kernel(
    tc, x_words, x_scales, d_words, d_scales, gn, w1_words, w1_scales, w2_words, w2_scales,
    offs, k1, n1, n2, two, n3, out_0, out_1, out_2,
):
    nc = tc.nc

    def words_in_hbm(words):
        return words[0].rearrange("p c r -> p (c r)").bitcast(I32)

    with ExitStack() as ctx:
        held = ctx.enter_context(tc.tile_pool(name="held", bufs=1))
        psum = ctx.enter_context(tc.psum_pool(name="psum", bufs=1))

        def load_list(src, name):
            tile = held.tile(list(src.shape), U16, name=name)
            nc.sync.dma_start(tile[:], src)
            return tile

        d_scale_table = held.tile([P, TABLE], U8, name="d_scale_table", tag="d_scales_then_w2_words", align_bytes=64)
        x_scale_table = held.tile([P, TABLE], U8, name="x_scale_table", align_bytes=64)
        nc.gpsimd.memset(x_scale_table[:].bitcast(I32), 0)

        k1_list = load_list(k1, "k1_list")
        d_scale_rows = d_scales[0].bitcast(I32)
        nc.sync.dma_start(
            d_scale_table[:].bitcast(I32), d_scale_rows.unsqueeze(1).to_broadcast([16, 8, TABLE // 4])
        )
        offs_list = load_list(offs, "offs_list")
        d_word_table = held.tile([P, TABLE], U32, name="d_word_table", align_bytes=64)
        x_word_table = held.tile([P, TABLE], U32, name="x_word_table", align_bytes=64)
        nc.sync.dma_start(d_word_table[:].bitcast(I32), words_in_hbm(d_words))
        x_scale_rows = x_scales[0].bitcast(I32)
        for q in range(4):
            nc.sync.dma_start(x_scale_table[32 * q : 32 * q + 4, :].bitcast(I32), x_scale_rows[4 * q : 4 * q + 4, :])
        nc.sync.dma_start(x_word_table[:].bitcast(I32), words_in_hbm(x_words))
        two_list = load_list(two, "two_list")
        n1_list = load_list(n1, "n1_list")
        n2_list = load_list(n2, "n2_list")
        n3_list = load_list(n3, "n3_list")
        gain = held.tile([P, PACK], F32, name="gain")
        nc.sync.dma_start(gain[:], gn.rearrange("(p t) o -> p (t o)", t=PACK))

        def gather_packed(table, offsets, dtype, name, tag=None):
            picked = held.tile([P, S], dtype, name=name, tag=tag or name, align_bytes=64)
            nc.vector.tensor_copy(picked[:], table[:].indirect(offsets[:]))
            return picked

        def dealt(tile):
            return tile.rearrange("p (m t) -> p t m", t=PACK)

        def by_tile(tile):
            return tile.rearrange("p (t m) -> p t m", t=PACK)

        def deal_words(engine_copy, dst, src):
            engine_copy(
                dst[:].rearrange("p (t c i) -> p c t i", t=PACK, i=4), src[:].rearrange("p (c i t) -> p c t i", t=PACK, i=4)
            )

        key_scales_picked = gather_packed(d_scale_table, k1_list, U8, "key_scales_picked", tag="key_scales_then_w1_words")
        key_scales_dealt = held.tile([P, S], U8, name="key_scales_dealt", tag="key_then_x2_scales", align_bytes=64)
        nc.vector.tensor_copy(by_tile(key_scales_dealt[:]), dealt(key_scales_picked[:]))
        key_scales = held.tile([P, S], U8, name="key_scales", align_bytes=64)
        nc.vector.tensor_copy(key_scales[:].bitcast(I32), key_scales_dealt[:].bitcast(I32))
        for r in range(1, 4):
            nc.scalar.dma_start(key_scales[r:P:32, :].bitcast(I32), key_scales_dealt[8 * r : P : 32, :].bitcast(I32))
        key_words_picked = gather_packed(d_word_table, k1_list, U32, "key_words_picked", tag="key_words_then_w_scales")
        key_words = held.tile([P, S], U32, name="key_words", align_bytes=64)
        deal_words(nc.vector.tensor_copy, key_words, key_words_picked)
        xq_scales = gather_packed(x_scale_table, offs_list, U8, "xq_scales")
        xq_words = gather_packed(x_word_table, offs_list, U32, "xq_words")

        score_banks = [psum.tile([P, S], F32, name=f"score_bank{t}") for t in range(PACK)]
        for t in range(PACK):
            cols = slice(P * t, P * (t + 1))
            nc.tensor.matmul_mx(
                out=score_banks[t][:], lhsT=key_words[:, cols].bitcast(FP8X4), lhsT_scale=key_scales[:, cols],
                rhs=xq_words[:].bitcast(FP8X4), rhs_scale=xq_scales[:], start=True, stop=True,
            )

        x2_scales = gather_packed(x_scale_table, two_list, U8, "x2_scales", tag="key_then_x2_scales")
        x2_words = gather_packed(x_word_table, two_list, U32, "x2_words")

        w2_raw = held.tile([P, S], U32, name="w2_raw", tag="d_scales_then_w2_words", align_bytes=64)
        w1_raw = held.tile([P, S], U32, name="w1_raw", tag="key_scales_then_w1_words", align_bytes=64)
        nc.gpsimd.dma_start(w2_raw[:].bitcast(I32), words_in_hbm(w2_words))
        nc.gpsimd.dma_start(w1_raw[:].bitcast(I32), words_in_hbm(w1_words))
        w1_dealt = held.tile([P, S], U32, name="w1_dealt", align_bytes=64)
        w2_dealt = held.tile([P, S], U32, name="w2_dealt", align_bytes=64)
        deal_words(nc.scalar.copy, w2_dealt, w2_raw)
        deal_words(nc.scalar.copy, w1_dealt, w1_raw)
        w_scales_raw = held.tile([P, S], U8, name="w_scales_raw", tag="key_words_then_w_scales", align_bytes=64)
        nc.gpsimd.memset(w_scales_raw[:], 0)
        for first, scales in ((0, w1_scales), (4, w2_scales)):
            rows = scales[0].bitcast(I32)
            for q in range(4):
                nc.sync.dma_start(
                    w_scales_raw[32 * q + first : 32 * q + first + 4, :].bitcast(I32), rows[4 * q : 4 * q + 4, :]
                )
        w_scales = held.tile([P, S], U8, name="w_scales", align_bytes=64)
        nc.gpsimd.tensor_copy(by_tile(w_scales[:]), dealt(w_scales_raw[:]))

        n_banks = S // BANK_COLS
        h_banks = [psum.tile([P, PACK, BANK_COLS], F32, name=f"h_bank{b}") for b in range(n_banks)]
        for b in range(n_banks):
            cols = slice(BANK_COLS * b, BANK_COLS * (b + 1))
            for t in range(PACK):
                rows = slice(P * t, P * (t + 1))
                nc.tensor.matmul_mx(
                    out=h_banks[b][:, t, :], lhsT=w2_dealt[:, rows].bitcast(FP8X4), lhsT_scale=w_scales[4:P, rows],
                    rhs=x2_words[:, cols].bitcast(FP8X4), rhs_scale=x2_scales[:, cols], start=(t == 0), stop=False,
                )

        scaled_gain = held.tile([P, PACK], F32, name="scaled_gain")
        nc.gpsimd.tensor_scalar(scaled_gain[:], gain[:], SCORE_SCALE, 0.0, ALU.mult, ALU.add)
        s_rows = [held.tile([P, S], F32, name=f"s_rows{t}") for t in range(PACK)]
        tanh_rows = [held.tile([P, S], F32, name=f"tanh_rows{t}") for t in range(PACK)]
        h_rows = [held.tile([P, H_WINDOW], F32, name=f"h_rows{t}") for t in range(PACK)]
        for t in range(PACK):
            nc.gpsimd.memset(h_rows[t][:, S:], 0.0)

        def round_interleaved(engine_copy, values, width, name):
            rounded = held.tile([P, width * PACK], BF16, name=name, align_bytes=64)
            engine_copy(
                rounded[:].rearrange("p (j t) -> p j t", t=PACK),
                values[:].rearrange("p t j -> p j t"),
            )
            return rounded

        for n, (start, width) in enumerate(Z_CHUNKS):
            cols = slice(start, start + width)
            entries = slice(start // 16, (start + width) // 16)
            z_values = held.tile([P, PACK, width], F32, name=f"z_values{n}")
            for t in range(PACK):
                if n == 0:
                    if t < 2:
                        nc.scalar.activation(s_rows[t][:], score_banks[t][:], ACT.Copy, scale=SCORE_SCALE)
                    else:
                        nc.vector.tensor_scalar(s_rows[t][:], score_banks[t][:], SCORE_SCALE, None, ALU.mult)
                    nc.scalar.activation(tanh_rows[t][:], score_banks[t][:], ACT.Tanh, scale=SCORE_SCALE)
                s_at_n1 = held.tile([P, width], F32, name=f"s_at_n1_{n}_{t}")
                if (n, t) == (1, 0):
                    nc.vector.tensor_copy(s_at_n1[:], s_rows[t][:].indirect(n1_list[:, entries]))
                else:
                    nc.scalar.activation(s_at_n1[:], s_rows[t][:].indirect(n1_list[:, entries]), ACT.Copy)
                pair = held.tile([P, width], F32, name=f"pair_{n}_{t}")
                nc.vector.tensor_tensor(pair[:], tanh_rows[t][:].indirect(n2_list[:, entries]), s_at_n1[:], ALU.mult)
                nc.vector.scalar_tensor_tensor(
                    z_values[:, t, :], score_banks[t][:, cols], scaled_gain[:, t : t + 1], pair[:], ALU.mult, ALU.mult
                )
            z_rounded = round_interleaved(
                nc.vector.tensor_copy if n == len(Z_CHUNKS) - 1 else nc.scalar.copy, z_values, width, f"z_rounded{n}")
            z_words = held.tile([P, width], U32, name=f"z_words{n}", align_bytes=64)
            z_scales = held.tile([P, width], U8, name=f"z_scales{n}", align_bytes=64)
            nc.vector.quantize_mx(out=z_words[:].bitcast(FP8X4), scales=z_scales[:], in_=z_rounded[:])
            for b in range(start // BANK_COLS, (start + width) // BANK_COLS):
                part = slice(BANK_COLS * b - start, BANK_COLS * (b + 1) - start)
                for t in range(PACK):
                    rows = slice(P * t, P * (t + 1))
                    nc.tensor.matmul_mx(
                        out=h_banks[b][:, t, :], lhsT=w1_dealt[:, rows].bitcast(FP8X4), lhsT_scale=w_scales[:, rows],
                        rhs=z_words[:, part].bitcast(FP8X4), rhs_scale=z_scales[:, part],
                        start=False, stop=(t == PACK - 1),
                    )
        for b in range(n_banks):
            for t in range(PACK):
                copy_out = nc.vector.tensor_copy if (b == n_banks - 1 and t > 0) else nc.scalar.copy
                copy_out(h_rows[t][:, BANK_COLS * b : BANK_COLS * (b + 1)], h_banks[b][:, t, :])

        out_rows = out_0.rearrange("(p t) j -> p t j", t=PACK)
        out_words_hbm = words_in_hbm(out_1)
        out_scales = held.tile([P, S], U8, name="out_scales", align_bytes=64)
        for n, (start, width) in enumerate(OUT_CHUNKS):
            cols = slice(start, start + width)
            entries = slice(start // 4, (start + width) // 4)
            members = held.tile([P, PACK, 4 * width], F32, name=f"members{n}")
            for t in range(PACK):
                looked_up = h_rows[t][:].indirect(n3_list[:, entries])
                if t == PACK - 1:
                    nc.vector.tensor_copy(members[:, t, :], looked_up)
                else:
                    nc.scalar.activation(members[:, t, :], looked_up, ACT.Copy)
            quads = members[:].rearrange("p t (u v m) -> p (t u) v m", v=2, m=4)
            pair_max = held.tile([P, PACK * width // 2, 2, 2], F32, name=f"pair_max{n}")
            nc.vector.tensor_tensor(
                pair_max[:].rearrange("p u m v -> p u v m"), quads[:, :, :, 0:2], quads[:, :, :, 2:4], ALU.max
            )
            largest = held.tile([P, PACK * width], F32, name=f"largest{n}")
            nc.vector.tensor_tensor(
                largest[:].rearrange("p (u v) -> p u v", v=2), pair_max[:, :, 0, :], pair_max[:, :, 1, :], ALU.max
            )
            result = held.tile([P, PACK, width], F32, name=f"result{n}")
            in_bank = slice(start % BANK_COLS, start % BANK_COLS + width)
            nc.vector.tensor_tensor(
                result[:], h_banks[start // BANK_COLS][:, :, in_bank],
                largest[:].rearrange("p (t j) -> p t j", t=PACK), ALU.subtract,
            )
            nc.sync.dma_start(out_rows[:, :, cols], result[:])
            rounded = round_interleaved(
                nc.vector.tensor_copy if n < 2 else nc.scalar.copy, result, width, f"out_rounded{n}"
            )
            out_words = held.tile([P, width], U32, name=f"out_words{n}", align_bytes=64)
            nc.vector.quantize_mx(out=out_words[:].bitcast(FP8X4), scales=out_scales[:, cols], in_=rounded[:])
            nc.sync.dma_start(out_words_hbm[:, cols], out_words[:].bitcast(I32))
        out_scale_rows = out_2[0].bitcast(I32)
        for q in range(4):
            queue = nc.scalar if q % 2 else nc.sync
            queue.dma_start(out_scale_rows[4 * q : 4 * q + 4, :], out_scales[32 * q : 32 * q + 4, :].bitcast(I32))
